import numpy as np
import ml_dtypes


def mxq(x, axis, fmt="e4m3"):
    dtype, down = {"e4m3": (ml_dtypes.float8_e4m3fn, 7), "e5m2": (ml_dtypes.float8_e5m2, 14)}[fmt]
    v = np.moveaxis(np.asarray(x, np.float32).astype(ml_dtypes.bfloat16).astype(np.float64), axis, -1)
    blocks = v.reshape(v.shape[:-1] + (-1, 32))
    amax = np.abs(blocks).max(-1, keepdims=True)
    byte = np.maximum(np.where(amax > 0, np.frexp(amax)[1] - 1 + 127, 0) - down, 1)
    scale = np.exp2(byte - 127.0)
    codes = (blocks / scale).astype(np.float32).astype(dtype).astype(np.float64)
    return np.moveaxis((codes * scale).reshape(v.shape), -1, axis)


WIDE = False


def mx_kscale(k):
    if not WIDE:
        return np.ones(k)
    levels = np.array([10, -10, 5, -5, 0])
    if k % 512:
        return np.exp2(np.random.permutation(np.resize(levels, k // 32))).repeat(32)
    a = np.empty((k // 512, 16))
    for p in range(k // 512):
        a[p, :8] = np.random.permutation(np.resize(levels, 8))
        for g in range(8):
            far = levels[np.abs(levels - a[p, g]) >= 10]
            a[p, g + 8] = far[np.random.randint(len(far))]
    return np.exp2(a.ravel()).repeat(32)


BF16 = ml_dtypes.bfloat16


def bf(x):
    return np.asarray(x, np.float32).astype(BF16)


def f64(x):
    return np.asarray(x).astype(np.float64)


E2M1 = np.array([0.0, 0.5, 1.0, 1.5, 2.0, 3.0, 4.0, 6.0, -0.0, -0.5, -1.0, -1.5, -2.0, -3.0, -4.0, -6.0])


def pack_weight(w, fmt):
    k, n = w.shape
    w = f64(bf(w)).reshape(k // 32, 32, n)
    amax = np.abs(w).max(1)
    if fmt == "e4m3":
        byte = np.frexp(amax)[1] - 1 + 127 - 7
    else:
        mant, ex = np.frexp(amax / 6.0)
        byte = np.where(mant > 0.5, ex, ex - 1) + 127
    byte = np.clip(np.where(amax > 0, byte, 1), 1, 254)
    scaled = (w * np.exp2(127.0 - byte)[:, None, :]).reshape(k, n).astype(np.float32)
    by_word = np.ascontiguousarray(scaled.reshape(k // 512, 128, 4, n).transpose(0, 1, 3, 2))
    if fmt == "e4m3":
        words = by_word.astype(ml_dtypes.float8_e4m3fn).view(np.uint8)
    else:
        c = by_word.astype(ml_dtypes.float4_e2m1fn).view(np.uint8) & 0xF
        words = c[..., 0::2] | (c[..., 1::2] << 4)
    return np.ascontiguousarray(words), np.ascontiguousarray(byte.astype(np.uint8).reshape(k // 512, 16, n))


def unpack_weight(words, scales, fmt):
    g, p, n, _ = words.shape
    if fmt == "e4m3":
        vals = np.ascontiguousarray(words).view(ml_dtypes.float8_e4m3fn).astype(np.float64)
    else:
        nib = np.empty((g, p, n, 4), np.uint8)
        nib[..., 0::2] = words & 0xF
        nib[..., 1::2] = words >> 4
        vals = E2M1[nib]
    vals = vals * np.repeat(np.exp2(scales.astype(np.float64) - 127.0), 8, axis=1)[..., None]
    return vals.transpose(0, 1, 3, 2).reshape(g * 512, n)
def pack4(w):
    words, scales = pack_weight(w, "e2m1")
    return words.reshape(words.shape[0], 128, -1), scales


def unpack4(words, scales):
    return unpack_weight(words.reshape(words.shape[0], 128, -1, 2), scales, "e2m1")


def planes(Y):
    n, m = Y.shape
    b = f64(bf(Y)).reshape(n // 32, 32, m)
    amax = np.abs(b).max(1)
    byte = np.clip(np.where(amax > 0, np.frexp(amax)[1] - 1 + 127 - 7, 1), 1, 254)
    codes = (b * np.exp2(127.0 - byte)[:, None, :]).reshape(n, m).astype(np.float32).astype(ml_dtypes.float8_e4m3fn).view(np.uint8)
    words = codes.reshape(n // 512, 128, 4, m).transpose(0, 1, 3, 2)
    return np.ascontiguousarray(words), np.ascontiguousarray(byte.astype(np.uint8).reshape(n // 512, 16, m))


G, R, K, F, P, C = 4, 512, 1024, 1024, 512, 512


def setup_inputs():
    s = mx_kscale(G * K)
    t = mx_kscale(G * F)
    x = np.random.randn(G, R, K) * s.reshape(G, 1, K)
    w = np.random.randn(G * K, F) / np.sqrt(K) / s[:, None]
    hidden_scale = (1.0 + 0.1 * np.random.randn(G, F)) * t.reshape(G, F)
    v = 1.2 * np.random.randn(G * F, C) / np.sqrt(F) / t[:, None]
    u = 1.2 * np.random.randn(G * P, C) / np.sqrt(P) / t.reshape(G, F)[:, :P].reshape(G * P, 1)
    bias = 0.3 * np.random.randn(G, C)
    gain = np.exp(0.8 * np.random.randn(G, C))
    w_words, w_scales = pack4(w)
    v_words, v_scales = pack4(v)
    u_words, u_scales = pack4(u)
    return {"x": bf(x), "w_words": w_words, "w_scales": w_scales,
            "hidden_scale": bf(hidden_scale),
            "v_words": v_words, "v_scales": v_scales,
            "u_words": u_words, "u_scales": u_scales,
            "bias": bf(bias), "gain": bf(gain)}

def reference(x, w_words, w_scales, hidden_scale, v_words, v_scales, u_words, u_scales, bias, gain):
    W = unpack4(w_words, w_scales).reshape(G, K, F)
    V = unpack4(v_words, v_scales).reshape(G, F, C)
    U = unpack4(u_words, u_scales).reshape(G, P, C)
    xq = mxq(f64(x), 2, "e4m3")
    z = xq @ W
    h = z / (1.0 + np.exp(-z)) * f64(hidden_scale)[:, None, :]
    hq = mxq(h, 2, "e4m3")
    full = hq @ V
    short = hq[:, :, :P] @ U
    y = np.tanh(full - short + f64(bias)[:, None, :]) * f64(gain)[:, None, :]
    Y = y.reshape(G * R, C).T
    words, scales = planes(Y)
    return y, words, scales

@@ -1,0 +1,392 @@
+from contextlib import ExitStack
+
+import concourse.mybir as mybir
+from concourse.masks import make_identity
+
+G, R, K, F, C = 4, 512, 1024, 1024, 512
+FLOPS = 2 * G * R * (K * F + F * C + 512 * C)
+
+F32 = mybir.dt.float32
+BF16 = mybir.dt.bfloat16
+I32 = mybir.dt.int32
+U32 = mybir.dt.uint32
+U8 = mybir.dt.uint8
+FP8X4 = mybir.dt.float8_e4m3fn_x4
+FP4X4 = mybir.dt.float4_e2m1fn_x4
+ACT = mybir.ActivationFunctionType
+ALU = mybir.AluOpType
+
+P = 128
+BIAS_ROW = 32
+GAIN_ROW = 36
+CONST_ROWS = 40
+
+
+def tile_matryoshka_head_gap_k7_kernel(
+    tc, x, w_words, w_scales, hidden_scale, v_words, v_scales, u_words, u_scales, bias, gain, out_0, out_1, out_2
+):
+    nc = tc.nc
+    with ExitStack() as ctx:
+        keep = ctx.enter_context(tc.tile_pool(name="keep", bufs=1))
+        one = ctx.enter_context(tc.tile_pool(name="one", bufs=1))
+        two = ctx.enter_context(tc.tile_pool(name="two", bufs=2))
+        psum = ctx.enter_context(tc.psum_pool(name="psum", bufs=1))
+        ctx.enter_context(tc.manual_schedule())
+
+        bank_count = [0]
+
+        def next_bank():
+            n = bank_count[0]
+            bank_count[0] = n + 1
+            return psum.tile([P, 512], F32, name="bank%d" % (n % 8))
+
+        def kept(name, shape, dtype):
+            return keep.tile(shape, dtype, name=name, align_bytes=64)
+
+        x_raw = [[kept("x_raw%d_%d" % (e, g), [P, 4, 512], BF16) for g in range(2)] for e in range(G)]
+        w_raw = [kept("w_raw%d" % e, [P, 2, 2 * F], U8) for e in range(G)]
+        ws_packed = kept("ws_packed", [P, F], U8)
+        ws_sorted = kept("ws_sorted", [P, F], U8)
+        ws_all = kept("ws_all", [P, 8, F], U8)
+        v_first = kept("v_first", [P, 2, 2 * C], U8)
+        v_rest = kept("v_rest", [P, 6, 2 * C], U8)
+        u_first = kept("u_first", [P, 1, 2 * C], U8)
+        u_rest = kept("u_rest", [P, 3, 2 * C], U8)
+        vs_all = kept("vs_all", [P, 8, C], U8)
+        us_all = kept("us_all", [P, 4, C], U8)
+        vec_raw = kept("vec_raw", [P, 512], BF16)
+        vec_rows = kept("vec_rows", [P, 512], F32)
+        vec_cols = kept("vec_cols", [P, CONST_ROWS, 4, 1], F32)
+        ident = kept("ident", [P, P], F32)
+        warm = kept("warm", [P, 2], F32)
+        y_scales = kept("y_scales", [P, G * R], U8)
+
+        def words_of(tile3):
+            return tile3[:].rearrange("p g n -> p (g n)").bitcast(I32)
+
+        def load_words(dst, src, g0, g1):
+            nc.sync.dma_start(out=dst[:].bitcast(I32), in_=src[g0:g1].rearrange("g p n -> p g n").bitcast(I32))
+
+        def load_scales(dst, src, g0, g1):
+            for r in range(4):
+                nc.sync.dma_start(
+                    out=dst[r:P:32].bitcast(I32),
+                    in_=src[g0:g1].rearrange("g (q r) n -> r q g n", r=4)[r].bitcast(I32),
+                )
+
+        def load_x(e, g):
+            nc.sync.dma_start(
+                out=x_raw[e][g][:],
+                in_=x[e].rearrange("(a p) k -> p a k", p=P)[:, :, 512 * g : 512 * (g + 1)],
+            )
+
+        nc.vector.memset(warm[:, 0:1], 0.0)
+        nc.vector.memset(words_of(ws_all), 0)
+        nc.vector.memset(vec_rows[:], 0.0)
+        nc.vector.memset(words_of(vs_all), 0)
+        nc.vector.memset(words_of(us_all), 0)
+        make_identity(nc, ident[:])
+        nc.scalar.activation(out=warm[:, 1:2], in_=warm[:, 0:1], func=ACT.Silu)
+
+        def v_codes(e, g):
+            return v_first[:, g, :] if e == 0 else v_rest[:, 2 * e - 2 + g, :]
+
+        def u_codes(e):
+            return u_first[:, 0, :] if e == 0 else u_rest[:, e - 1, :]
+
+        st = {}
+
+        def sort_w_codes(e, gf):
+            dst = kept("w_codes%d_%d" % (e, gf), [P, 2, 4, 128, 2], U8)
+            src = w_raw[e][:, :, 1024 * gf : 1024 * (gf + 1)].rearrange("p g (m t b) -> p g t m b", t=4, b=2)
+            nc.vector.tensor_copy(out=dst[:], in_=src)
+            st["wc", e, gf] = dst
+
+        def sort_w_scales():
+            nc.vector.tensor_copy(
+                out=ws_sorted[:].rearrange("p (gf t m) -> p gf t m", gf=2, t=4),
+                in_=ws_packed[:].rearrange("p (gf m t) -> p gf t m", gf=2, t=4),
+            )
+            for q in range(4):
+                nc.sync.dma_start(
+                    out=ws_all[32 * q : 32 * q + 4].bitcast(I32), in_=ws_sorted[32 * q : 32 * q + 32, :].bitcast(I32)
+                )
+
+        def turn_x(e, g):
+            grouped = one.tile([P, R, 4], BF16, name="x_grouped%d" % g, align_bytes=64)
+            dst = grouped[:].rearrange("p r t -> p (r t)").bitcast(F32).rearrange("p (a r u) -> p a r u", a=4, u=2)
+            words = x_raw[e][g][:].bitcast(F32)
+            for half in range(2):
+                bank = next_bank()
+                for a2 in range(2):
+                    for u in range(2):
+                        col = 256 * a2 + 128 * u
+                        nc.tensor.transpose(bank[:, col : col + 128], words[:, 2 * half + a2, u:256:2], ident[:])
+                nc.scalar.copy(
+                    out=dst[:, 2 * half : 2 * half + 2],
+                    in_=bank[:].rearrange("p (a u r) -> p a r u", a=2, u=2),
+                )
+            st["xg", e, g] = grouped
+
+        def quantize(name, pool, grouped):
+            codes = pool.tile([P, R], U32, name=name + "_codes", align_bytes=64)
+            scales = pool.tile([P, R], U8, name=name + "_scales", align_bytes=64)
+            nc.vector.quantize_mx(
+                out=codes[:].bitcast(FP8X4), scales=scales[:], in_=grouped[:].rearrange("p r t -> p (r t)")
+            )
+            return codes, scales
+
+        def quantize_x(e, g):
+            st["xq", e, g] = quantize("xq%d" % g, two, st["xg", e, g])
+
+        def project(e, gf):
+            act = one.tile([P, 4, R], F32, name="act%d" % gf)
+            for t in range(4):
+                bank = next_bank()
+                for g in range(2):
+                    codes, scales = st["xq", e, g]
+                    nc.tensor.matmul_mx(
+                        out=bank[:],
+                        lhsT=st["wc", e, gf][:, g, t].rearrange("p m b -> p (m b)").bitcast(FP4X4),
+                        lhsT_scale=ws_all[:, 2 * e + g, 512 * gf + 128 * t : 512 * gf + 128 * (t + 1)],
+                        rhs=codes[:].bitcast(FP8X4),
+                        rhs_scale=scales[:],
+                        start=(g == 0),
+                        stop=(g == 1),
+                    )
+                nc.scalar.activation(out=act[:, t, :], in_=bank[:], func=ACT.Silu)
+            st["act", e, gf] = act
+
+        def scale_hidden(e, gf):
+            grouped = one.tile([P, R, 4], BF16, name="h_grouped%d" % gf, align_bytes=64)
+            row = 2 * e + gf
+            nc.vector.tensor_tensor(
+                out=grouped[:].rearrange("p (c i) t -> p c t i", i=4),
+                in0=st["act", e, gf][:].rearrange("p t (c i) -> p c t i", i=4),
+                in1=vec_cols[:, row : row + 1, :, :].to_broadcast([P, R // 4, 4, 4]),
+                op=ALU.mult,
+            )
+            st["hg", e, gf] = grouped
+
+        def negate_hidden(e):
+            grouped = one.tile([P, R, 4], BF16, name="h_negated", align_bytes=64)
+            nc.vector.tensor_scalar(
+                out=grouped[:].rearrange("p r t -> p (r t)"),
+                in0=st["hg", e, 0][:].rearrange("p r t -> p (r t)"),
+                scalar1=-1.0,
+                scalar2=None,
+                op0=ALU.mult,
+            )
+            st["hg", e, 2] = grouped
+
+        def quantize_h(e, which):
+            st["hq", e, which] = quantize("hq%d" % which, two, st["hg", e, which])
+
+        def head_pass(bank, codes, scales, j, hq, start, stop):
+            nc.tensor.matmul_mx(
+                out=bank[:],
+                lhsT=codes[:, 256 * j : 256 * (j + 1)].bitcast(FP4X4),
+                lhsT_scale=scales[:, 128 * j : 128 * (j + 1)],
+                rhs=hq[0][:].bitcast(FP8X4),
+                rhs_scale=hq[1][:],
+                start=start,
+                stop=stop,
+            )
+
+        def heads(e):
+            soft = one.tile([P, 4, R], F32, name="soft")
+            banks = [next_bank() for j in range(4)]
+            for j in range(4):
+                head_pass(banks[j], v_codes(e, 0), vs_all[:, 2 * e, :], j, st["hq", e, 0], True, False)
+            for j in range(4):
+                head_pass(banks[j], u_codes(e), us_all[:, e, :], j, st["hq", e, 2], False, False)
+                head_pass(banks[j], v_codes(e, 1), vs_all[:, 2 * e + 1, :], j, st["hq", e, 1], False, True)
+                nc.scalar.activation(
+                    out=soft[:, j, :], in_=banks[j][:], func=ACT.Tanh, bias=vec_cols[:, BIAS_ROW + e, j, :]
+                )
+            st["soft", e] = soft
+            y_cols = one.tile([P, 4, R], F32, name="y_cols")
+            st["yc", e] = y_cols
+
+        def apply_gain(e, j):
+            nc.vector.tensor_scalar(
+                out=st["yc", e][:, j, :],
+                in0=st["soft", e][:, j, :],
+                scalar1=vec_cols[:, GAIN_ROW + e, j, :],
+                scalar2=None,
+                op0=ALU.mult,
+            )
+
+        def turn_y(e, a, copy_out):
+            rows = two.tile([P, C], F32, name="y_rows%d" % a)
+            bank = next_bank()
+            for j in range(4):
+                nc.tensor.transpose(
+                    bank[:, 128 * j : 128 * (j + 1)], st["yc", e][:, j, 128 * a : 128 * (a + 1)], ident[:]
+                )
+            copy_out(out=rows[:], in_=bank[:])
+            nc.sync.dma_start(out=out_0[e, 128 * a : 128 * (a + 1), :], in_=rows[:])
+            st["yr", e, a] = rows
+
+        def round_y(e, a, copy):
+            if a % 2 == 0:
+                pairs = two.tile([P, 2, 512], BF16, name="y_pairs%d" % (a // 2))
+                st["yp", e, a // 2] = pairs
+            copy(
+                out=st["yp", e, a // 2][:, a % 2, :].rearrange("p (u m i) -> p u m i", u=2, i=2),
+                in_=st["yr", e, a][:].rearrange("p (m u i) -> p u m i", u=2, i=2),
+            )
+
+        def turn_pairs(e, half):
+            grouped = one.tile([P, 256, 4], BF16, name="y_grouped%d" % half, align_bytes=64)
+            dst = grouped[:].rearrange("p r t -> p (r t)").bitcast(F32).rearrange("p (a r u) -> p a r u", a=2, u=2)
+            words = st["yp", e, half][:].rearrange("p a n -> p (a n)").bitcast(F32)
+            bank = next_bank()
+            for i in range(4):
+                nc.tensor.transpose(bank[:, 128 * i : 128 * (i + 1)], words[:, 128 * i : 128 * (i + 1)], ident[:])
+            nc.scalar.copy(out=dst, in_=bank[:].rearrange("p (a u r) -> p a r u", a=2, u=2))
+            st["yg", e, half] = grouped
+
+        def quantize_y(e, half):
+            codes = two.tile([P, 256], U32, name="y_codes%d" % half, align_bytes=64)
+            m0 = R * e + 256 * half
+            nc.vector.quantize_mx(
+                out=codes[:].bitcast(FP8X4),
+                scales=y_scales[:, m0 : m0 + 256],
+                in_=st["yg", e, half][:].rearrange("p r t -> p (r t)"),
+            )
+            nc.sync.dma_start(
+                out=out_1[0].rearrange("p m t -> p (m t)")[:, 4 * m0 : 4 * (m0 + 256)].bitcast(I32),
+                in_=codes[:].bitcast(I32),
+            )
+
+        def widen_vectors():
+            nc.scalar.copy(
+                out=vec_rows[0:8, :].rearrange("p (t m) -> p t m", t=4),
+                in_=vec_raw[0:8, :].rearrange("p (m t) -> p t m", t=4),
+            )
+            nc.scalar.copy(out=vec_rows[BIAS_ROW:CONST_ROWS, :], in_=vec_raw[BIAS_ROW:CONST_ROWS, :])
+
+        def turn_vectors():
+            bank = next_bank()
+            for i in range(4):
+                nc.tensor.transpose(bank[:, 128 * i : 128 * (i + 1)], vec_rows[:, 128 * i : 128 * (i + 1)], ident[:])
+            nc.scalar.copy(
+                out=vec_cols[:].rearrange("p row i o -> p row (i o)"),
+                in_=bank[:].rearrange("p (i row) -> p row i", i=4)[:, 0:CONST_ROWS, :],
+            )
+
+        nc.sync.dma_start(out=ws_packed[:].bitcast(I32), in_=w_scales.rearrange("g q n -> q g n").bitcast(I32))
+        load_x(0, 0)
+        load_words(w_raw[0], w_words, 0, 2)
+        load_x(0, 1)
+        load_x(1, 0)
+        nc.sync.dma_start(out=vec_raw[0:8, :], in_=hidden_scale.rearrange("e (g n) -> (e g) n", g=2))
+        nc.sync.dma_start(out=vec_raw[BIAS_ROW : BIAS_ROW + 4, :], in_=bias)
+        nc.sync.dma_start(out=vec_raw[GAIN_ROW : GAIN_ROW + 4, :], in_=gain)
+        sort_w_scales()
+        load_words(w_raw[1], w_words, 2, 4)
+        load_x(1, 1)
+        load_words(w_raw[2], w_words, 4, 6)
+        load_words(v_first, v_words, 0, 2)
+        load_words(u_first, u_words, 0, 1)
+        load_scales(vs_all, v_scales, 0, 8)
+        load_scales(us_all, u_scales, 0, 4)
+        load_x(2, 0)
+        load_x(2, 1)
+        load_words(w_raw[3], w_words, 6, 8)
+        load_words(v_rest, v_words, 2, 8)
+        load_words(u_rest, u_words, 1, 4)
+        load_x(3, 0)
+        load_x(3, 1)
+
+        s_copy, v_copy = nc.scalar.copy, nc.vector.tensor_copy
+        turn_x(0, 0)
+        sort_w_codes(0, 0)
+        sort_w_codes(0, 1)
+        quantize_x(0, 0)
+        turn_x(0, 1)
+        widen_vectors()
+        turn_x(1, 0)
+        quantize_x(0, 1)
+        sort_w_codes(1, 0)
+        project(0, 0)
+        turn_vectors()
+        turn_x(1, 1)
+        sort_w_codes(1, 1)
+        quantize_x(1, 0)
+        sort_w_codes(2, 0)
+        project(0, 1)
+        scale_hidden(0, 0)
+        quantize_x(1, 1)
+        negate_hidden(0)
+        quantize_h(0, 0)
+        scale_hidden(0, 1)
+        quantize_h(0, 2)
+        quantize_h(0, 1)
+
+        for e in range(G - 1):
+            far = e + 2 < G
+            project(e + 1, 0)
+            heads(e)
+            scale_hidden(e + 1, 0)
+            for j in range(4):
+                apply_gain(e, j)
+            project(e + 1, 1)
+            negate_hidden(e + 1)
+            quantize_h(e + 1, 0)
+            if far:
+                sort_w_codes(e + 2, 1)
+                turn_x(e + 2, 0)
+                turn_x(e + 2, 1)
+            else:
+                quantize_h(e + 1, 2)
+            scale_hidden(e + 1, 1)
+            if far:
+                quantize_x(e + 2, 0)
+                quantize_x(e + 2, 1)
+                quantize_h(e + 1, 2)
+            quantize_h(e + 1, 1)
+            for a in range(4):
+                turn_y(e, a, s_copy)
+            if e > 0:
+                turn_pairs(e - 1, 0)
+                turn_pairs(e - 1, 1)
+            for a in range(4):
+                round_y(e, a, v_copy)
+            if far:
+                if e > 0:
+                    quantize_y(e - 1, 0)
+                    quantize_y(e - 1, 1)
+                if e == 0:
+                    sort_w_codes(3, 0)
+            else:
+                quantize_y(e - 1, 0)
+                quantize_y(e - 1, 1)
+
+        e = G - 1
+        heads(e)
+        turn_pairs(e - 1, 0)
+        turn_pairs(e - 1, 1)
+        for j in range(4):
+            apply_gain(e, j)
+        quantize_y(e - 1, 0)
+        quantize_y(e - 1, 1)
+        turn_y(e, 0, s_copy)
+        turn_y(e, 1, v_copy)
+        turn_y(e, 2, s_copy)
+        round_y(e, 0, v_copy)
+        turn_y(e, 3, s_copy)
+        round_y(e, 1, v_copy)
+        round_y(e, 2, v_copy)
+        turn_pairs(e, 0)
+        round_y(e, 3, v_copy)
+        turn_pairs(e, 1)
+        quantize_y(e, 0)
+        quantize_y(e, 1)
+
+        for r in range(4):
+            nc.sync.dma_start(
+                out=out_2[0].rearrange("(q r) m -> r q m", r=4)[r].bitcast(I32),
+                in_=y_scales[r:P:32, :].bitcast(I32),
+            )

@@ -47,7 +47,7 @@ def tile_matryoshka_head_gap_k7_kernel(
         w_raw = [kept("w_raw%d" % e, [P, 2, 2 * F], U8) for e in range(G)]
         ws_packed = kept("ws_packed", [P, F], U8)
         ws_sorted = kept("ws_sorted", [P, F], U8)
-        ws_all = kept("ws_all", [P, 8, F], U8)
+        ws_half = [kept("ws_half%d" % half, [P, 4, F], U8) for half in range(2)]
         v_first = kept("v_first", [P, 2, 2 * C], U8)
         v_rest = kept("v_rest", [P, 6, 2 * C], U8)
         u_first = kept("u_first", [P, 1, 2 * C], U8)
@@ -81,10 +81,11 @@ def tile_matryoshka_head_gap_k7_kernel(
             )
 
         nc.vector.memset(warm[:, 0:1], 0.0)
-        nc.vector.memset(words_of(ws_all), 0)
+        nc.vector.memset(words_of(ws_half[0]), 0)
         nc.vector.memset(vec_rows[:], 0.0)
         nc.vector.memset(words_of(vs_all), 0)
         nc.vector.memset(words_of(us_all), 0)
+        nc.vector.memset(words_of(ws_half[1]), 0)
         make_identity(nc, ident[:])
         nc.scalar.activation(out=warm[:, 1:2], in_=warm[:, 0:1], func=ACT.Silu)
 
@@ -102,14 +103,23 @@ def tile_matryoshka_head_gap_k7_kernel(
             nc.vector.tensor_copy(out=dst[:], in_=src)
             st["wc", e, gf] = dst
 
+        def load_packed_scales(half):
+            nc.sync.dma_start(
+                out=ws_packed[64 * half : 64 * (half + 1), :].bitcast(I32),
+                in_=w_scales[4 * half : 4 * (half + 1)].rearrange("g q n -> q g n").bitcast(I32),
+            )
+
         def sort_w_scales():
             nc.vector.tensor_copy(
                 out=ws_sorted[:].rearrange("p (gf t m) -> p gf t m", gf=2, t=4),
                 in_=ws_packed[:].rearrange("p (gf m t) -> p gf t m", gf=2, t=4),
             )
+
+        def spread_w_scales(half):
             for q in range(4):
+                p0 = 64 * half + 16 * q
                 nc.sync.dma_start(
-                    out=ws_all[32 * q : 32 * q + 4].bitcast(I32), in_=ws_sorted[32 * q : 32 * q + 32, :].bitcast(I32)
+                    out=ws_half[half][32 * q : 32 * q + 4].bitcast(I32), in_=ws_sorted[p0 : p0 + 16, :].bitcast(I32)
                 )
 
         def turn_x(e, g):
@@ -148,7 +158,7 @@ def tile_matryoshka_head_gap_k7_kernel(
                     nc.tensor.matmul_mx(
                         out=bank[:],
                         lhsT=st["wc", e, gf][:, g, t].rearrange("p m b -> p (m b)").bitcast(FP4X4),
-                        lhsT_scale=ws_all[:, 2 * e + g, 512 * gf + 128 * t : 512 * gf + 128 * (t + 1)],
+                        lhsT_scale=ws_half[e // 2][:, 2 * (e % 2) + g, 512 * gf + 128 * t : 512 * gf + 128 * (t + 1)],
                         rhs=codes[:].bitcast(FP8X4),
                         rhs_scale=scales[:],
                         start=(g == 0),
@@ -161,9 +171,9 @@ def tile_matryoshka_head_gap_k7_kernel(
             grouped = one.tile([P, R, 4], BF16, name="h_grouped%d" % gf, align_bytes=64)
             row = 2 * e + gf
             nc.vector.tensor_tensor(
-                out=grouped[:].rearrange("p (c i) t -> p c t i", i=4),
-                in0=st["act", e, gf][:].rearrange("p t (c i) -> p c t i", i=4),
-                in1=vec_cols[:, row : row + 1, :, :].to_broadcast([P, R // 4, 4, 4]),
+                out=grouped[:].rearrange("p (c i) t -> p c t i", i=2),
+                in0=st["act", e, gf][:].rearrange("p t (c i) -> p c t i", i=2),
+                in1=vec_cols[:, row : row + 1, :, :].to_broadcast([P, R // 2, 4, 2]),
                 op=ALU.mult,
             )
             st["hg", e, gf] = grouped
@@ -193,25 +203,34 @@ def tile_matryoshka_head_gap_k7_kernel(
                 stop=stop,
             )
 
-        def heads(e):
+        def soften(e, j, rows):
+            nc.scalar.activation(
+                out=st["soft", e][:, j, rows],
+                in_=st["logits", e][j][:, rows],
+                func=ACT.Tanh,
+                bias=vec_cols[:, BIAS_ROW + e, j, :],
+            )
+
+        def heads(e, rows, late):
             soft = one.tile([P, 4, R], F32, name="soft")
+            y_cols = one.tile([P, 4, R], F32, name="y_cols")
             banks = [next_bank() for j in range(4)]
+            st["soft", e], st["yc", e], st["logits", e] = soft, y_cols, banks
             for j in range(4):
                 head_pass(banks[j], v_codes(e, 0), vs_all[:, 2 * e, :], j, st["hq", e, 0], True, False)
-            for j in range(4):
                 head_pass(banks[j], u_codes(e), us_all[:, e, :], j, st["hq", e, 2], False, False)
-                head_pass(banks[j], v_codes(e, 1), vs_all[:, 2 * e + 1, :], j, st["hq", e, 1], False, True)
-                nc.scalar.activation(
-                    out=soft[:, j, :], in_=banks[j][:], func=ACT.Tanh, bias=vec_cols[:, BIAS_ROW + e, j, :]
-                )
-            st["soft", e] = soft
-            y_cols = one.tile([P, 4, R], F32, name="y_cols")
-            st["yc", e] = y_cols
+                if not late:
+                    head_pass(banks[j], v_codes(e, 1), vs_all[:, 2 * e + 1, :], j, st["hq", e, 1], False, True)
+                    soften(e, j, rows)
+            if late:
+                for j in range(4):
+                    head_pass(banks[j], v_codes(e, 1), vs_all[:, 2 * e + 1, :], j, st["hq", e, 1], False, True)
+                    soften(e, j, rows)
 
-        def apply_gain(e, j):
+        def apply_gain(e, j, rows):
             nc.vector.tensor_scalar(
-                out=st["yc", e][:, j, :],
-                in0=st["soft", e][:, j, :],
+                out=st["yc", e][:, j, rows],
+                in0=st["soft", e][:, j, rows],
                 scalar1=vec_cols[:, GAIN_ROW + e, j, :],
                 scalar2=None,
                 op0=ALU.mult,
@@ -228,35 +247,36 @@ def tile_matryoshka_head_gap_k7_kernel(
             nc.sync.dma_start(out=out_0[e, 128 * a : 128 * (a + 1), :], in_=rows[:])
             st["yr", e, a] = rows
 
-        def round_y(e, a, copy):
-            if a % 2 == 0:
-                pairs = two.tile([P, 2, 512], BF16, name="y_pairs%d" % (a // 2))
-                st["yp", e, a // 2] = pairs
-            copy(
-                out=st["yp", e, a // 2][:, a % 2, :].rearrange("p (u m i) -> p u m i", u=2, i=2),
+        def round_y(e, a):
+            pairs = two.tile([P, 512], BF16, name="y_pairs%d" % a)
+            nc.vector.tensor_copy(
+                out=pairs[:].rearrange("p (u m i) -> p u m i", u=2, i=2),
                 in_=st["yr", e, a][:].rearrange("p (m u i) -> p u m i", u=2, i=2),
             )
+            st["yp", e, a] = pairs
 
-        def turn_pairs(e, half):
-            grouped = one.tile([P, 256, 4], BF16, name="y_grouped%d" % half, align_bytes=64)
-            dst = grouped[:].rearrange("p r t -> p (r t)").bitcast(F32).rearrange("p (a r u) -> p a r u", a=2, u=2)
-            words = st["yp", e, half][:].rearrange("p a n -> p (a n)").bitcast(F32)
+        def turn_pairs(e, a0, n):
+            grouped = two.tile([P, 128 * n, 4], BF16, name="y_grouped%d" % a0, align_bytes=64)
+            dst = grouped[:].rearrange("p r t -> p (r t)").bitcast(F32).rearrange("p (a r u) -> p a r u", a=n, u=2)
             bank = next_bank()
-            for i in range(4):
-                nc.tensor.transpose(bank[:, 128 * i : 128 * (i + 1)], words[:, 128 * i : 128 * (i + 1)], ident[:])
-            nc.scalar.copy(out=dst, in_=bank[:].rearrange("p (a u r) -> p a r u", a=2, u=2))
-            st["yg", e, half] = grouped
+            for a in range(n):
+                words = st["yp", e, a0 + a][:].bitcast(F32)
+                for u in range(2):
+                    col = 256 * a + 128 * u
+                    nc.tensor.transpose(bank[:, col : col + 128], words[:, 128 * u : 128 * (u + 1)], ident[:])
+            nc.scalar.copy(out=dst, in_=bank[:, 0 : 256 * n].rearrange("p (a u r) -> p a r u", a=n, u=2))
+            st["yg", e, a0] = grouped
 
-        def quantize_y(e, half):
-            codes = two.tile([P, 256], U32, name="y_codes%d" % half, align_bytes=64)
-            m0 = R * e + 256 * half
+        def quantize_y(e, a0, n):
+            codes = two.tile([P, 128 * n], U32, name="y_codes%d" % a0, align_bytes=64)
+            m0 = R * e + 128 * a0
             nc.vector.quantize_mx(
                 out=codes[:].bitcast(FP8X4),
-                scales=y_scales[:, m0 : m0 + 256],
-                in_=st["yg", e, half][:].rearrange("p r t -> p (r t)"),
+                scales=y_scales[:, m0 : m0 + 128 * n],
+                in_=st["yg", e, a0][:].rearrange("p r t -> p (r t)"),
             )
             nc.sync.dma_start(
-                out=out_1[0].rearrange("p m t -> p (m t)")[:, 4 * m0 : 4 * (m0 + 256)].bitcast(I32),
+                out=out_1[0].rearrange("p m t -> p (m t)")[:, 4 * m0 : 4 * (m0 + 128 * n)].bitcast(I32),
                 in_=codes[:].bitcast(I32),
             )
 
@@ -276,15 +296,17 @@ def tile_matryoshka_head_gap_k7_kernel(
                 in_=bank[:].rearrange("p (i row) -> p row i", i=4)[:, 0:CONST_ROWS, :],
             )
 
-        nc.sync.dma_start(out=ws_packed[:].bitcast(I32), in_=w_scales.rearrange("g q n -> q g n").bitcast(I32))
+        load_packed_scales(0)
+        load_packed_scales(1)
         load_x(0, 0)
         load_words(w_raw[0], w_words, 0, 2)
         load_x(0, 1)
         load_x(1, 0)
         nc.sync.dma_start(out=vec_raw[0:8, :], in_=hidden_scale.rearrange("e (g n) -> (e g) n", g=2))
+        sort_w_scales()
+        spread_w_scales(0)
         nc.sync.dma_start(out=vec_raw[BIAS_ROW : BIAS_ROW + 4, :], in_=bias)
         nc.sync.dma_start(out=vec_raw[GAIN_ROW : GAIN_ROW + 4, :], in_=gain)
-        sort_w_scales()
         load_words(w_raw[1], w_words, 2, 4)
         load_x(1, 1)
         load_words(w_raw[2], w_words, 4, 6)
@@ -292,6 +314,7 @@ def tile_matryoshka_head_gap_k7_kernel(
         load_words(u_first, u_words, 0, 1)
         load_scales(vs_all, v_scales, 0, 8)
         load_scales(us_all, u_scales, 0, 4)
+        spread_w_scales(1)
         load_x(2, 0)
         load_x(2, 1)
         load_words(w_raw[3], w_words, 6, 8)
@@ -321,69 +344,72 @@ def tile_matryoshka_head_gap_k7_kernel(
         quantize_x(1, 1)
         negate_hidden(0)
         quantize_h(0, 0)
-        scale_hidden(0, 1)
         quantize_h(0, 2)
+        scale_hidden(0, 1)
+        sort_w_codes(2, 1)
         quantize_h(0, 1)
 
+        all_rows = slice(0, R)
         for e in range(G - 1):
             far = e + 2 < G
             project(e + 1, 0)
-            heads(e)
+            heads(e, all_rows, e == 0)
             scale_hidden(e + 1, 0)
             for j in range(4):
-                apply_gain(e, j)
-            project(e + 1, 1)
+                apply_gain(e, j, all_rows)
             negate_hidden(e + 1)
             quantize_h(e + 1, 0)
             if far:
-                sort_w_codes(e + 2, 1)
                 turn_x(e + 2, 0)
                 turn_x(e + 2, 1)
-            else:
-                quantize_h(e + 1, 2)
-            scale_hidden(e + 1, 1)
-            if far:
                 quantize_x(e + 2, 0)
+            quantize_h(e + 1, 2)
+            if far:
                 quantize_x(e + 2, 1)
-                quantize_h(e + 1, 2)
-            quantize_h(e + 1, 1)
+            if e == 0:
+                sort_w_codes(3, 0)
+            project(e + 1, 1)
+            scale_hidden(e + 1, 1)
             for a in range(4):
                 turn_y(e, a, s_copy)
             if e > 0:
-                turn_pairs(e - 1, 0)
-                turn_pairs(e - 1, 1)
-            for a in range(4):
-                round_y(e, a, v_copy)
+                turn_pairs(e - 1, 0, 2)
+                turn_pairs(e - 1, 2, 2)
             if far:
-                if e > 0:
-                    quantize_y(e - 1, 0)
-                    quantize_y(e - 1, 1)
-                if e == 0:
-                    sort_w_codes(3, 0)
-            else:
-                quantize_y(e - 1, 0)
-                quantize_y(e - 1, 1)
+                round_y(e, 0)
+            quantize_h(e + 1, 1)
+            for a in range(1 if far else 0, 4):
+                round_y(e, a)
+            if e > 0:
+                quantize_y(e - 1, 0, 2)
+                quantize_y(e - 1, 2, 2)
+            if e == 0:
+                sort_w_codes(3, 1)
 
         e = G - 1
-        heads(e)
-        turn_pairs(e - 1, 0)
-        turn_pairs(e - 1, 1)
+        low, high = slice(0, R // 2), slice(R // 2, R)
+        heads(e, low, True)
         for j in range(4):
-            apply_gain(e, j)
-        quantize_y(e - 1, 0)
-        quantize_y(e - 1, 1)
-        turn_y(e, 0, s_copy)
-        turn_y(e, 1, v_copy)
+            apply_gain(e, j, low)
+        for j in range(4):
+            soften(e, j, high)
+            apply_gain(e, j, high)
+        turn_y(e, 0, v_copy)
+        turn_y(e, 1, s_copy)
         turn_y(e, 2, s_copy)
-        round_y(e, 0, v_copy)
-        turn_y(e, 3, s_copy)
-        round_y(e, 1, v_copy)
-        round_y(e, 2, v_copy)
-        turn_pairs(e, 0)
-        round_y(e, 3, v_copy)
-        turn_pairs(e, 1)
-        quantize_y(e, 0)
-        quantize_y(e, 1)
+        round_y(e, 0)
+        round_y(e, 1)
+        turn_y(e, 3, v_copy)
+        turn_pairs(e - 1, 0, 2)
+        turn_pairs(e, 0, 2)
+        round_y(e, 2)
+        round_y(e, 3)
+        turn_pairs(e - 1, 2, 2)
+        quantize_y(e - 1, 0, 2)
+        turn_pairs(e, 2, 2)
+        quantize_y(e, 0, 2)
+        quantize_y(e - 1, 2, 2)
+        quantize_y(e, 2, 2)
 
         for r in range(4):
             nc.sync.dma_start(

from contextlib import ExitStack

import concourse.mybir as mybir
from concourse.masks import make_identity

G, R, K, F, C = 4, 512, 1024, 1024, 512
FLOPS = 2 * G * R * (K * F + F * C + 512 * C)

F32 = mybir.dt.float32
BF16 = mybir.dt.bfloat16
I32 = mybir.dt.int32
U32 = mybir.dt.uint32
U8 = mybir.dt.uint8
FP8X4 = mybir.dt.float8_e4m3fn_x4
FP4X4 = mybir.dt.float4_e2m1fn_x4
ACT = mybir.ActivationFunctionType
ALU = mybir.AluOpType

P = 128
BIAS_ROW = 32
GAIN_ROW = 36
CONST_ROWS = 40


def tile_matryoshka_head_gap_k7_kernel(
    tc, x, w_words, w_scales, hidden_scale, v_words, v_scales, u_words, u_scales, bias, gain, out_0, out_1, out_2
):
    nc = tc.nc
    with ExitStack() as ctx:
        keep = ctx.enter_context(tc.tile_pool(name="keep", bufs=1))
        one = ctx.enter_context(tc.tile_pool(name="one", bufs=1))
        two = ctx.enter_context(tc.tile_pool(name="two", bufs=2))
        psum = ctx.enter_context(tc.psum_pool(name="psum", bufs=1))
        ctx.enter_context(tc.manual_schedule())

        bank_count = [0]

        def next_bank():
            n = bank_count[0]
            bank_count[0] = n + 1
            return psum.tile([P, 512], F32, name="bank%d" % (n % 8))

        def kept(name, shape, dtype):
            return keep.tile(shape, dtype, name=name, align_bytes=64)

        x_raw = [[kept("x_raw%d_%d" % (e, g), [P, 4, 512], BF16) for g in range(2)] for e in range(G)]
        w_raw = [kept("w_raw%d" % e, [P, 2, 2 * F], U8) for e in range(G)]
        ws_packed = kept("ws_packed", [P, F], U8)
        ws_sorted = kept("ws_sorted", [P, F], U8)
        ws_half = [kept("ws_half%d" % half, [P, 4, F], U8) for half in range(2)]
        v_first = kept("v_first", [P, 2, 2 * C], U8)
        v_rest = kept("v_rest", [P, 6, 2 * C], U8)
        u_first = kept("u_first", [P, 1, 2 * C], U8)
        u_rest = kept("u_rest", [P, 3, 2 * C], U8)
        vs_all = kept("vs_all", [P, 8, C], U8)
        us_all = kept("us_all", [P, 4, C], U8)
        vec_raw = kept("vec_raw", [P, 512], BF16)
        vec_rows = kept("vec_rows", [P, 512], F32)
        vec_cols = kept("vec_cols", [P, CONST_ROWS, 4, 1], F32)
        ident = kept("ident", [P, P], F32)
        warm = kept("warm", [P, 2], F32)
        y_scales = kept("y_scales", [P, G * R], U8)

        def words_of(tile3):
            return tile3[:].rearrange("p g n -> p (g n)").bitcast(I32)

        def load_words(dst, src, g0, g1):
            nc.sync.dma_start(out=dst[:].bitcast(I32), in_=src[g0:g1].rearrange("g p n -> p g n").bitcast(I32))

        def load_scales(dst, src, g0, g1):
            for r in range(4):
                nc.sync.dma_start(
                    out=dst[r:P:32].bitcast(I32),
                    in_=src[g0:g1].rearrange("g (q r) n -> r q g n", r=4)[r].bitcast(I32),
                )

        def load_x(e, g):
            nc.sync.dma_start(
                out=x_raw[e][g][:],
                in_=x[e].rearrange("(a p) k -> p a k", p=P)[:, :, 512 * g : 512 * (g + 1)],
            )

        nc.vector.memset(warm[:, 0:1], 0.0)
        nc.vector.memset(words_of(ws_half[0]), 0)
        nc.vector.memset(vec_rows[:], 0.0)
        nc.vector.memset(words_of(vs_all), 0)
        nc.vector.memset(words_of(us_all), 0)
        nc.vector.memset(words_of(ws_half[1]), 0)
        make_identity(nc, ident[:])
        nc.scalar.activation(out=warm[:, 1:2], in_=warm[:, 0:1], func=ACT.Silu)

        def v_codes(e, g):
            return v_first[:, g, :] if e == 0 else v_rest[:, 2 * e - 2 + g, :]

        def u_codes(e):
            return u_first[:, 0, :] if e == 0 else u_rest[:, e - 1, :]

        st = {}

        def sort_w_codes(e, gf):
            dst = kept("w_codes%d_%d" % (e, gf), [P, 2, 4, 128, 2], U8)
            src = w_raw[e][:, :, 1024 * gf : 1024 * (gf + 1)].rearrange("p g (m t b) -> p g t m b", t=4, b=2)
            nc.vector.tensor_copy(out=dst[:], in_=src)
            st["wc", e, gf] = dst

        def load_packed_scales(half):
            nc.sync.dma_start(
                out=ws_packed[64 * half : 64 * (half + 1), :].bitcast(I32),
                in_=w_scales[4 * half : 4 * (half + 1)].rearrange("g q n -> q g n").bitcast(I32),
            )

        def sort_w_scales():
            nc.vector.tensor_copy(
                out=ws_sorted[:].rearrange("p (gf t m) -> p gf t m", gf=2, t=4),
                in_=ws_packed[:].rearrange("p (gf m t) -> p gf t m", gf=2, t=4),
            )

        def spread_w_scales(half):
            for q in range(4):
                p0 = 64 * half + 16 * q
                nc.sync.dma_start(
                    out=ws_half[half][32 * q : 32 * q + 4].bitcast(I32), in_=ws_sorted[p0 : p0 + 16, :].bitcast(I32)
                )

        def turn_x(e, g):
            grouped = one.tile([P, R, 4], BF16, name="x_grouped%d" % g, align_bytes=64)
            dst = grouped[:].rearrange("p r t -> p (r t)").bitcast(F32).rearrange("p (a r u) -> p a r u", a=4, u=2)
            words = x_raw[e][g][:].bitcast(F32)
            for half in range(2):
                bank = next_bank()
                for a2 in range(2):
                    for u in range(2):
                        col = 256 * a2 + 128 * u
                        nc.tensor.transpose(bank[:, col : col + 128], words[:, 2 * half + a2, u:256:2], ident[:])
                nc.scalar.copy(
                    out=dst[:, 2 * half : 2 * half + 2],
                    in_=bank[:].rearrange("p (a u r) -> p a r u", a=2, u=2),
                )
            st["xg", e, g] = grouped

        def quantize(name, pool, grouped):
            codes = pool.tile([P, R], U32, name=name + "_codes", align_bytes=64)
            scales = pool.tile([P, R], U8, name=name + "_scales", align_bytes=64)
            nc.vector.quantize_mx(
                out=codes[:].bitcast(FP8X4), scales=scales[:], in_=grouped[:].rearrange("p r t -> p (r t)")
            )
            return codes, scales

        def quantize_x(e, g):
            st["xq", e, g] = quantize("xq%d" % g, two, st["xg", e, g])

        def project(e, gf):
            act = one.tile([P, 4, R], F32, name="act%d" % gf)
            for t in range(4):
                bank = next_bank()
                for g in range(2):
                    codes, scales = st["xq", e, g]
                    nc.tensor.matmul_mx(
                        out=bank[:],
                        lhsT=st["wc", e, gf][:, g, t].rearrange("p m b -> p (m b)").bitcast(FP4X4),
                        lhsT_scale=ws_half[e // 2][:, 2 * (e % 2) + g, 512 * gf + 128 * t : 512 * gf + 128 * (t + 1)],
                        rhs=codes[:].bitcast(FP8X4),
                        rhs_scale=scales[:],
                        start=(g == 0),
                        stop=(g == 1),
                    )
                nc.scalar.activation(out=act[:, t, :], in_=bank[:], func=ACT.Silu)
            st["act", e, gf] = act

        def scale_hidden(e, gf):
            grouped = one.tile([P, R, 4], BF16, name="h_grouped%d" % gf, align_bytes=64)
            row = 2 * e + gf
            nc.vector.tensor_tensor(
                out=grouped[:].rearrange("p (c i) t -> p c t i", i=2),
                in0=st["act", e, gf][:].rearrange("p t (c i) -> p c t i", i=2),
                in1=vec_cols[:, row : row + 1, :, :].to_broadcast([P, R // 2, 4, 2]),
                op=ALU.mult,
            )
            st["hg", e, gf] = grouped

        def negate_hidden(e):
            grouped = one.tile([P, R, 4], BF16, name="h_negated", align_bytes=64)
            nc.vector.tensor_scalar(
                out=grouped[:].rearrange("p r t -> p (r t)"),
                in0=st["hg", e, 0][:].rearrange("p r t -> p (r t)"),
                scalar1=-1.0,
                scalar2=None,
                op0=ALU.mult,
            )
            st["hg", e, 2] = grouped

        def quantize_h(e, which):
            st["hq", e, which] = quantize("hq%d" % which, two, st["hg", e, which])

        def head_pass(bank, codes, scales, j, hq, start, stop):
            nc.tensor.matmul_mx(
                out=bank[:],
                lhsT=codes[:, 256 * j : 256 * (j + 1)].bitcast(FP4X4),
                lhsT_scale=scales[:, 128 * j : 128 * (j + 1)],
                rhs=hq[0][:].bitcast(FP8X4),
                rhs_scale=hq[1][:],
                start=start,
                stop=stop,
            )

        def soften(e, j, rows):
            nc.scalar.activation(
                out=st["soft", e][:, j, rows],
                in_=st["logits", e][j][:, rows],
                func=ACT.Tanh,
                bias=vec_cols[:, BIAS_ROW + e, j, :],
            )

        def heads(e, rows, late):
            soft = one.tile([P, 4, R], F32, name="soft")
            y_cols = one.tile([P, 4, R], F32, name="y_cols")
            banks = [next_bank() for j in range(4)]
            st["soft", e], st["yc", e], st["logits", e] = soft, y_cols, banks
            for j in range(4):
                head_pass(banks[j], v_codes(e, 0), vs_all[:, 2 * e, :], j, st["hq", e, 0], True, False)
                head_pass(banks[j], u_codes(e), us_all[:, e, :], j, st["hq", e, 2], False, False)
                if not late:
                    head_pass(banks[j], v_codes(e, 1), vs_all[:, 2 * e + 1, :], j, st["hq", e, 1], False, True)
                    soften(e, j, rows)
            if late:
                for j in range(4):
                    head_pass(banks[j], v_codes(e, 1), vs_all[:, 2 * e + 1, :], j, st["hq", e, 1], False, True)
                    soften(e, j, rows)

        def apply_gain(e, j, rows):
            nc.vector.tensor_scalar(
                out=st["yc", e][:, j, rows],
                in0=st["soft", e][:, j, rows],
                scalar1=vec_cols[:, GAIN_ROW + e, j, :],
                scalar2=None,
                op0=ALU.mult,
            )

        def turn_y(e, a, copy_out):
            rows = two.tile([P, C], F32, name="y_rows%d" % a)
            bank = next_bank()
            for j in range(4):
                nc.tensor.transpose(
                    bank[:, 128 * j : 128 * (j + 1)], st["yc", e][:, j, 128 * a : 128 * (a + 1)], ident[:]
                )
            copy_out(out=rows[:], in_=bank[:])
            nc.sync.dma_start(out=out_0[e, 128 * a : 128 * (a + 1), :], in_=rows[:])
            st["yr", e, a] = rows

        def round_y(e, a):
            pairs = two.tile([P, 512], BF16, name="y_pairs%d" % a)
            nc.vector.tensor_copy(
                out=pairs[:].rearrange("p (u m i) -> p u m i", u=2, i=2),
                in_=st["yr", e, a][:].rearrange("p (m u i) -> p u m i", u=2, i=2),
            )
            st["yp", e, a] = pairs

        def turn_pairs(e, a0, n):
            grouped = two.tile([P, 128 * n, 4], BF16, name="y_grouped%d" % a0, align_bytes=64)
            dst = grouped[:].rearrange("p r t -> p (r t)").bitcast(F32).rearrange("p (a r u) -> p a r u", a=n, u=2)
            bank = next_bank()
            for a in range(n):
                words = st["yp", e, a0 + a][:].bitcast(F32)
                for u in range(2):
                    col = 256 * a + 128 * u
                    nc.tensor.transpose(bank[:, col : col + 128], words[:, 128 * u : 128 * (u + 1)], ident[:])
            nc.scalar.copy(out=dst, in_=bank[:, 0 : 256 * n].rearrange("p (a u r) -> p a r u", a=n, u=2))
            st["yg", e, a0] = grouped

        def quantize_y(e, a0, n):
            codes = two.tile([P, 128 * n], U32, name="y_codes%d" % a0, align_bytes=64)
            m0 = R * e + 128 * a0
            nc.vector.quantize_mx(
                out=codes[:].bitcast(FP8X4),
                scales=y_scales[:, m0 : m0 + 128 * n],
                in_=st["yg", e, a0][:].rearrange("p r t -> p (r t)"),
            )
            nc.sync.dma_start(
                out=out_1[0].rearrange("p m t -> p (m t)")[:, 4 * m0 : 4 * (m0 + 128 * n)].bitcast(I32),
                in_=codes[:].bitcast(I32),
            )

        def widen_vectors():
            nc.scalar.copy(
                out=vec_rows[0:8, :].rearrange("p (t m) -> p t m", t=4),
                in_=vec_raw[0:8, :].rearrange("p (m t) -> p t m", t=4),
            )
            nc.scalar.copy(out=vec_rows[BIAS_ROW:CONST_ROWS, :], in_=vec_raw[BIAS_ROW:CONST_ROWS, :])

        def turn_vectors():
            bank = next_bank()
            for i in range(4):
                nc.tensor.transpose(bank[:, 128 * i : 128 * (i + 1)], vec_rows[:, 128 * i : 128 * (i + 1)], ident[:])
            nc.scalar.copy(
                out=vec_cols[:].rearrange("p row i o -> p row (i o)"),
                in_=bank[:].rearrange("p (i row) -> p row i", i=4)[:, 0:CONST_ROWS, :],
            )

        load_packed_scales(0)
        load_packed_scales(1)
        load_x(0, 0)
        load_words(w_raw[0], w_words, 0, 2)
        load_x(0, 1)
        load_x(1, 0)
        nc.sync.dma_start(out=vec_raw[0:8, :], in_=hidden_scale.rearrange("e (g n) -> (e g) n", g=2))
        sort_w_scales()
        spread_w_scales(0)
        nc.sync.dma_start(out=vec_raw[BIAS_ROW : BIAS_ROW + 4, :], in_=bias)
        nc.sync.dma_start(out=vec_raw[GAIN_ROW : GAIN_ROW + 4, :], in_=gain)
        load_words(w_raw[1], w_words, 2, 4)
        load_x(1, 1)
        load_words(w_raw[2], w_words, 4, 6)
        load_words(v_first, v_words, 0, 2)
        load_words(u_first, u_words, 0, 1)
        load_scales(vs_all, v_scales, 0, 8)
        load_scales(us_all, u_scales, 0, 4)
        spread_w_scales(1)
        load_x(2, 0)
        load_x(2, 1)
        load_words(w_raw[3], w_words, 6, 8)
        load_words(v_rest, v_words, 2, 8)
        load_words(u_rest, u_words, 1, 4)
        load_x(3, 0)
        load_x(3, 1)

        s_copy, v_copy = nc.scalar.copy, nc.vector.tensor_copy
        turn_x(0, 0)
        sort_w_codes(0, 0)
        sort_w_codes(0, 1)
        quantize_x(0, 0)
        turn_x(0, 1)
        widen_vectors()
        turn_x(1, 0)
        quantize_x(0, 1)
        sort_w_codes(1, 0)
        project(0, 0)
        turn_vectors()
        turn_x(1, 1)
        sort_w_codes(1, 1)
        quantize_x(1, 0)
        sort_w_codes(2, 0)
        project(0, 1)
        scale_hidden(0, 0)
        quantize_x(1, 1)
        negate_hidden(0)
        quantize_h(0, 0)
        quantize_h(0, 2)
        scale_hidden(0, 1)
        sort_w_codes(2, 1)
        quantize_h(0, 1)

        all_rows = slice(0, R)
        for e in range(G - 1):
            far = e + 2 < G
            project(e + 1, 0)
            heads(e, all_rows, e == 0)
            scale_hidden(e + 1, 0)
            for j in range(4):
                apply_gain(e, j, all_rows)
            negate_hidden(e + 1)
            quantize_h(e + 1, 0)
            if far:
                turn_x(e + 2, 0)
                turn_x(e + 2, 1)
                quantize_x(e + 2, 0)
            quantize_h(e + 1, 2)
            if far:
                quantize_x(e + 2, 1)
            if e == 0:
                sort_w_codes(3, 0)
            project(e + 1, 1)
            scale_hidden(e + 1, 1)
            for a in range(4):
                turn_y(e, a, s_copy)
            if e > 0:
                turn_pairs(e - 1, 0, 2)
                turn_pairs(e - 1, 2, 2)
            if far:
                round_y(e, 0)
            quantize_h(e + 1, 1)
            for a in range(1 if far else 0, 4):
                round_y(e, a)
            if e > 0:
                quantize_y(e - 1, 0, 2)
                quantize_y(e - 1, 2, 2)
            if e == 0:
                sort_w_codes(3, 1)

        e = G - 1
        low, high = slice(0, R // 2), slice(R // 2, R)
        heads(e, low, True)
        for j in range(4):
            apply_gain(e, j, low)
        for j in range(4):
            soften(e, j, high)
            apply_gain(e, j, high)
        turn_y(e, 0, v_copy)
        turn_y(e, 1, s_copy)
        turn_y(e, 2, s_copy)
        round_y(e, 0)
        round_y(e, 1)
        turn_y(e, 3, v_copy)
        turn_pairs(e - 1, 0, 2)
        turn_pairs(e, 0, 2)
        round_y(e, 2)
        round_y(e, 3)
        turn_pairs(e - 1, 2, 2)
        quantize_y(e - 1, 0, 2)
        turn_pairs(e, 2, 2)
        quantize_y(e, 0, 2)
        quantize_y(e - 1, 2, 2)
        quantize_y(e, 2, 2)

        for r in range(4):
            nc.sync.dma_start(
                out=out_2[0].rearrange("(q r) m -> r q m", r=4)[r].bitcast(I32),
                in_=y_scales[r:P:32, :].bitcast(I32),
            )
